import numpy as np
import ml_dtypes


def mxq(x, axis, fmt="e4m3"):
    dtype, down = {"e4m3": (ml_dtypes.float8_e4m3fn, 7), "e5m2": (ml_dtypes.float8_e5m2, 14)}[fmt]
    v = np.moveaxis(np.asarray(x, np.float32).astype(ml_dtypes.bfloat16).astype(np.float64), axis, -1)
    blocks = v.reshape(v.shape[:-1] + (-1, 32))
    amax = np.abs(blocks).max(-1, keepdims=True)
    byte = np.maximum(np.where(amax > 0, np.frexp(amax)[1] - 1 + 127, 0) - down, 1)
    scale = np.exp2(byte - 127.0)
    codes = (blocks / scale).astype(np.float32).astype(dtype).astype(np.float64)
    return np.moveaxis((codes * scale).reshape(v.shape), -1, axis)


WIDE = False


def mx_kscale(k):
    if not WIDE:
        return np.ones(k)
    levels = np.array([10, -10, 5, -5, 0])
    if k % 512:
        return np.exp2(np.random.permutation(np.resize(levels, k // 32))).repeat(32)
    a = np.empty((k // 512, 16))
    for p in range(k // 512):
        a[p, :8] = np.random.permutation(np.resize(levels, 8))
        for g in range(8):
            far = levels[np.abs(levels - a[p, g]) >= 10]
            a[p, g + 8] = far[np.random.randint(len(far))]
    return np.exp2(a.ravel()).repeat(32)


def f64(x):
    return np.asarray(x).astype(np.float64)


def striped(idx):
    return np.tile(idx.reshape(-1, 16).T, (8, 1)).astype(np.uint16)


def unstriped(offs):
    return offs[:16].T.reshape(-1).astype(np.int64)


def relu(v):
    return np.maximum(v, 0.0)


K, T, E, C, N = 512, 512, 8, 128, 512


def by_expert(wq, xq):
    return np.concatenate([wq[e].T @ xq[:, e * C:(e + 1) * C] for e in range(E)], axis=1)


def setup_inputs():
    n = np.random.standard_normal
    s = mx_kscale(K)[:, None]
    first = np.random.permutation(np.repeat(np.arange(E), T // E))
    second = (first + 1 + np.random.permutation(np.repeat(np.arange(E - 1), -(-T // (E - 1)))[:T])) % E
    while np.bincount(second, minlength=E).max() != T // E:
        load = np.bincount(second, minlength=E); hi, lo = int(load.argmax()), int(load.argmin())
        t = np.flatnonzero((second == hi) & (first != lo))[0]; second[t] = lo
    slot_token = np.empty(E * C, np.int64); pos = np.empty((2, T), np.int64); fill = np.zeros(E, np.int64)
    place = np.stack([np.random.permutation(C) for _ in range(E)])
    for r, deal in enumerate((first, second)):
        for t in np.random.permutation(T):
            e = deal[t]; j = e * C + place[e, fill[e]]; fill[e] += 1; slot_token[j] = t; pos[r, t] = j
    g = np.random.uniform(0.2, 0.8, T)
    return {
        "xT": (n((K, T)) * s).astype(np.float32),
        "w": (n((E, K, N)) / np.sqrt(K) / s[None]).astype(np.float32),
        "b": (0.3 * n((N, E))).astype(np.float32),
        "gate": np.stack([np.tile(g, (N, 1)), np.tile(1.0 - g, (N, 1))]).astype(np.float32),
        "offs": striped(slot_token),
        "pos1": striped(pos[0]),
        "pos2": striped(pos[1]),
    }


def reference(xT, w, b, gate, offs, pos1, pos2):
    idx = unstriped(offs)
    xq = mxq(f64(xT)[:, idx], 0, "e4m3")
    y = by_expert(mxq(f64(w), 1, "e4m3"), xq)
    y = relu(y + np.repeat(f64(b), C, axis=1))
    return f64(gate[0]) * y[:, unstriped(pos1)] + f64(gate[1]) * y[:, unstriped(pos2)]

@@ -1,0 +1,163 @@
+from contextlib import ExitStack
+
+import concourse.mybir as mybir
+
+F32 = mybir.dt.float32
+BF16 = mybir.dt.bfloat16
+U32 = mybir.dt.uint32
+U16 = mybir.dt.uint16
+U8 = mybir.dt.uint8
+FP8X4 = mybir.dt.float8_e4m3fn_x4
+MULT = mybir.AluOpType.mult
+ADD = mybir.AluOpType.add
+RELU = mybir.ActivationFunctionType.Relu
+
+K, T, E, C, N = 512, 512, 8, 128, 512
+FLOPS = 2 * K * N * E * C
+P = 128
+PACK = 4
+BLOCKS = N // P
+
+VECTOR_X = 224
+VECTOR_SHARE = 3
+WHOLE = 4
+GATHER_CUTS = (0, 384, 768, 1024)
+
+
+def interleave(nc, grouped, raw, cut, width):
+    def view(out, src):
+        return out, src.rearrange("p t w -> p w t")
+
+    if cut > 0:
+        out, src = view(grouped[:, 0:cut, :], raw[:, :, 0:cut])
+        nc.vector.tensor_copy(out=out, in_=src)
+    if cut < width:
+        out, src = view(grouped[:, cut:width, :], raw[:, :, cut:width])
+        nc.scalar.copy(out=out, in_=src)
+
+
+def tile_routed_moe_kernel(tc, xT, w, b, gate, offs, pos1, pos2, out):
+    nc = tc.nc
+    with ExitStack() as ctx:
+        lists = ctx.enter_context(tc.tile_pool(name="lists", bufs=1))
+        keep = ctx.enter_context(tc.tile_pool(name="keep", bufs=1))
+        psum = ctx.enter_context(tc.psum_pool(name="psum", bufs=8))
+
+        offs_sb = lists.tile([P, E * C // 16], U16, name="offs_sb")
+        pos1_sb = lists.tile([P, T // 16], U16, name="pos1_sb")
+        pos2_sb = lists.tile([P, T // 16], U16, name="pos2_sb")
+        bias = lists.tile([P, BLOCKS, E], F32, name="bias")
+
+        pieces = [(e, 0, N) for e in range(WHOLE)]
+        pieces += [(e, 0, N // 2) for e in range(WHOLE, E)]
+        first_half = len(pieces)
+        pieces += [(e, N // 2, N) for e in range(WHOLE, E)]
+
+        x_raw = keep.tile([P, PACK, T], F32, name="x_raw")
+        nc.sync.dma_start(out=x_raw[:], in_=xT.rearrange("(p j) w -> p j w", j=PACK))
+        nc.sync.dma_start(out=offs_sb[:], in_=offs)
+        raws = []
+        gates = []
+
+        def load_gate(t):
+            g = keep.tile([P, 2, T], F32, name=f"gate{t}")
+            nc.sync.dma_start(out=g[:], in_=gate[:, t * P : (t + 1) * P, :].rearrange("r p n -> p r n"))
+            gates.append(g)
+
+        for i, (e, f0, f1) in enumerate(pieces):
+            if i == first_half:
+                for t in range(BLOCKS // 2):
+                    load_gate(t)
+            raw = keep.tile([P, PACK, f1 - f0], F32, name=f"w_raw{i}")
+            nc.sync.dma_start(out=raw[:], in_=w[e].rearrange("(p j) n -> p j n", j=PACK)[:, :, f0:f1])
+            raws.append(raw)
+            if i == 0:
+                nc.sync.dma_start(out=bias[:], in_=b.rearrange("(t p) e -> p t e", p=P))
+            if i == 2:
+                nc.sync.dma_start(out=pos1_sb[:], in_=pos1)
+                nc.sync.dma_start(out=pos2_sb[:], in_=pos2)
+        while len(gates) < BLOCKS:
+            load_gate(len(gates))
+
+        x_codes = keep.tile([P, T], U32, name="x_codes", align_bytes=64)
+        x_scales = keep.tile([P, T], U8, name="x_scales", align_bytes=64)
+        nc.gpsimd.memset(x_scales[:], 0)
+        x_grouped = keep.tile([P, T, PACK], BF16, name="x_grouped", align_bytes=64)
+        interleave(nc, x_grouped, x_raw, VECTOR_X, T)
+        nc.vector.quantize_mx(
+            out=x_codes[:].bitcast(FP8X4),
+            scales=x_scales[:],
+            in_=x_grouped[:].rearrange("p w j -> p (w j)"),
+        )
+        slot_codes = keep.tile([P, E * C], U32, name="slot_codes", align_bytes=64)
+        slot_scales = keep.tile([P, E * C], U8, name="slot_scales", align_bytes=64)
+
+        def gather(i):
+            a, z = GATHER_CUTS[i], GATHER_CUTS[i + 1]
+            part = offs_sb[:, a // 16 : z // 16]
+            nc.vector.tensor_copy(out=slot_codes[:, a:z], in_=x_codes[:].indirect(part))
+            nc.vector.tensor_copy(out=slot_scales[:, a:z], in_=x_scales[:].indirect(part))
+
+        ys = [keep.tile([P, E * C], F32, name=f"y{t}") for t in range(BLOCKS)]
+        codes = {}
+        grouped = {}
+
+        def convert(i):
+            e, f0, f1 = pieces[i]
+            width = f1 - f0
+            g = keep.tile([P, width, PACK], BF16, name=f"w_grouped{i}", align_bytes=64)
+            interleave(nc, g, raws[i], width * VECTOR_SHARE // 16, width)
+            grouped[i] = g
+
+        def quantise(i):
+            e, f0, f1 = pieces[i]
+            width = f1 - f0
+            c = keep.tile([P, width], U32, name=f"w_codes{i}", align_bytes=64)
+            s = keep.tile([P, width], U8, name=f"w_scales{i}", align_bytes=64)
+            nc.vector.quantize_mx(
+                out=c[:].bitcast(FP8X4),
+                scales=s[:],
+                in_=grouped[i][:].rearrange("p w j -> p (w j)"),
+            )
+            codes[i] = (c, s)
+
+        def multiply(i):
+            e, f0, f1 = pieces[i]
+            c, s = codes[i]
+            slots = slice(e * C, (e + 1) * C)
+            for f in range(f0, f1, P):
+                t = f // P
+                cols = slice(f - f0, f - f0 + P)
+                acc = psum.tile([P, C], F32, name="acc")
+                nc.tensor.matmul_mx(
+                    out=acc[:],
+                    lhsT=c[:, cols].bitcast(FP8X4),
+                    lhsT_scale=s[:, cols],
+                    rhs=slot_codes[:, slots].bitcast(FP8X4),
+                    rhs_scale=slot_scales[:, slots],
+                    start=True,
+                    stop=True,
+                )
+                nc.scalar.activation(ys[t][:, slots], acc[:], RELU, bias=bias[:, t, e : e + 1])
+
+        def combine(t):
+            first = keep.tile([P, T], F32, name=f"first{t}")
+            second = keep.tile([P, T], F32, name=f"second{t}")
+            nc.vector.tensor_tensor(first[:], ys[t][:].indirect(pos1_sb[:]), gates[t][:, 0, :], MULT)
+            nc.vector.tensor_tensor(second[:], ys[t][:].indirect(pos2_sb[:]), gates[t][:, 1, :], MULT)
+            total = keep.tile([P, T], F32, name=f"total{t}")
+            nc.vector.tensor_tensor(total[:], first[:], second[:], ADD)
+            nc.sync.dma_start(out=out[t * P : (t + 1) * P, :], in_=total[:])
+
+        for i in range(len(GATHER_CUTS) - 1):
+            gather(i)
+        for i in range(len(pieces) + 1):
+            if i < len(pieces):
+                convert(i)
+            if i > 0:
+                quantise(i - 1)
+                multiply(i - 1)
+            if i == first_half:
+                pass
+        for t in range(BLOCKS):
+            combine(t)

@@ -18,15 +18,18 @@ P = 128
 PACK = 4
 BLOCKS = N // P
 
-VECTOR_X = 224
-VECTOR_SHARE = 3
-WHOLE = 4
+VECTOR_X = 256
+VECTOR_SHARES = (9, 0)
+WHOLE = 8
 GATHER_CUTS = (0, 384, 768, 1024)
 
 
 def interleave(nc, grouped, raw, cut, width):
     def view(out, src):
-        return out, src.rearrange("p t w -> p w t")
+        return (
+            out.rearrange("p (c i) t -> p c t i", i=4),
+            src.rearrange("p t (c i) -> p c t i", i=4),
+        )
 
     if cut > 0:
         out, src = view(grouped[:, 0:cut, :], raw[:, :, 0:cut])
@@ -106,7 +109,7 @@ def tile_routed_moe_kernel(tc, xT, w, b, gate, offs, pos1, pos2, out):
             e, f0, f1 = pieces[i]
             width = f1 - f0
             g = keep.tile([P, width, PACK], BF16, name=f"w_grouped{i}", align_bytes=64)
-            interleave(nc, g, raws[i], width * VECTOR_SHARE // 16, width)
+            interleave(nc, g, raws[i], width * VECTOR_SHARES[i >= first_half] // 16, width)
             grouped[i] = g
 
         def quantise(i):
@@ -140,24 +143,31 @@ def tile_routed_moe_kernel(tc, xT, w, b, gate, offs, pos1, pos2, out):
                 )
                 nc.scalar.activation(ys[t][:, slots], acc[:], RELU, bias=bias[:, t, e : e + 1])
 
-        def combine(t):
-            first = keep.tile([P, T], F32, name=f"first{t}")
-            second = keep.tile([P, T], F32, name=f"second{t}")
-            nc.vector.tensor_tensor(first[:], ys[t][:].indirect(pos1_sb[:]), gates[t][:, 0, :], MULT)
-            nc.vector.tensor_tensor(second[:], ys[t][:].indirect(pos2_sb[:]), gates[t][:, 1, :], MULT)
+        def fetch(t, r):
+            product = keep.tile([P, T], F32, name=f"product{t}_{r}")
+            pos = (pos1_sb, pos2_sb)[r]
+            nc.vector.tensor_tensor(product[:], ys[t][:].indirect(pos[:]), gates[t][:, r, :], MULT)
+            products[t, r] = product
+
+        def finish(t):
             total = keep.tile([P, T], F32, name=f"total{t}")
-            nc.vector.tensor_tensor(total[:], first[:], second[:], ADD)
+            nc.vector.tensor_tensor(total[:], products[t, 0][:], products[t, 1][:], ADD)
             nc.sync.dma_start(out=out[t * P : (t + 1) * P, :], in_=total[:])
 
-        for i in range(len(GATHER_CUTS) - 1):
-            gather(i)
-        for i in range(len(pieces) + 1):
-            if i < len(pieces):
+        products = {}
+        gather(0)
+        for i in range(E + 2):
+            if i < E:
                 convert(i)
-            if i > 0:
+            if 1 <= i < len(GATHER_CUTS) - 1:
+                gather(i)
+            if 1 <= i <= E:
                 quantise(i - 1)
-                multiply(i - 1)
-            if i == first_half:
-                pass
+            if i >= 2:
+                multiply(i - 2)
         for t in range(BLOCKS):
-            combine(t)
+            fetch(t, 0)
+            if t > 0:
+                finish(t - 1)
+            fetch(t, 1)
+        finish(BLOCKS - 1)

@@ -18,25 +18,17 @@ P = 128
 PACK = 4
 BLOCKS = N // P
 
-VECTOR_X = 256
-VECTOR_SHARES = (9, 0)
-WHOLE = 8
+VECTOR_TOKENS = 320
+SCALAR_EXPERTS = (0, 1)
+HALF = N // 2
 GATHER_CUTS = (0, 384, 768, 1024)
 
 
-def interleave(nc, grouped, raw, cut, width):
-    def view(out, src):
-        return (
-            out.rearrange("p (c i) t -> p c t i", i=4),
-            src.rearrange("p t (c i) -> p c t i", i=4),
-        )
-
-    if cut > 0:
-        out, src = view(grouped[:, 0:cut, :], raw[:, :, 0:cut])
-        nc.vector.tensor_copy(out=out, in_=src)
-    if cut < width:
-        out, src = view(grouped[:, cut:width, :], raw[:, :, cut:width])
-        nc.scalar.copy(out=out, in_=src)
+def interleave(copy, grouped, raw):
+    copy(
+        out=grouped.rearrange("p (c i) t -> p c t i", i=4),
+        in_=raw.rearrange("p t (c i) -> p c t i", i=4),
+    )
 
 
 def tile_routed_moe_kernel(tc, xT, w, b, gate, offs, pos1, pos2, out):
@@ -51,42 +43,35 @@ def tile_routed_moe_kernel(tc, xT, w, b, gate, offs, pos1, pos2, out):
         pos2_sb = lists.tile([P, T // 16], U16, name="pos2_sb")
         bias = lists.tile([P, BLOCKS, E], F32, name="bias")
 
-        pieces = [(e, 0, N) for e in range(WHOLE)]
-        pieces += [(e, 0, N // 2) for e in range(WHOLE, E)]
-        first_half = len(pieces)
-        pieces += [(e, N // 2, N) for e in range(WHOLE, E)]
-
         x_raw = keep.tile([P, PACK, T], F32, name="x_raw")
         nc.sync.dma_start(out=x_raw[:], in_=xT.rearrange("(p j) w -> p j w", j=PACK))
         nc.sync.dma_start(out=offs_sb[:], in_=offs)
         raws = []
-        gates = []
-
-        def load_gate(t):
-            g = keep.tile([P, 2, T], F32, name=f"gate{t}")
-            nc.sync.dma_start(out=g[:], in_=gate[:, t * P : (t + 1) * P, :].rearrange("r p n -> p r n"))
-            gates.append(g)
-
-        for i, (e, f0, f1) in enumerate(pieces):
-            if i == first_half:
-                for t in range(BLOCKS // 2):
-                    load_gate(t)
-            raw = keep.tile([P, PACK, f1 - f0], F32, name=f"w_raw{i}")
-            nc.sync.dma_start(out=raw[:], in_=w[e].rearrange("(p j) n -> p j n", j=PACK)[:, :, f0:f1])
+        for e in range(E):
+            raw = keep.tile([P, PACK, N], F32, name=f"w_raw{e}")
+            rows = w[e].rearrange("(p j) n -> p j n", j=PACK)
+            for a, z in ((0, HALF), (HALF, N)) if e == E - 1 else ((0, N),):
+                nc.sync.dma_start(out=raw[:, :, a:z], in_=rows[:, :, a:z])
             raws.append(raw)
-            if i == 0:
+            if e == 0:
                 nc.sync.dma_start(out=bias[:], in_=b.rearrange("(t p) e -> p t e", p=P))
-            if i == 2:
+            if e == E - 2:
                 nc.sync.dma_start(out=pos1_sb[:], in_=pos1)
                 nc.sync.dma_start(out=pos2_sb[:], in_=pos2)
-        while len(gates) < BLOCKS:
-            load_gate(len(gates))
+        gates = {}
+        for t in range(BLOCKS):
+            for r in range(2):
+                g = keep.tile([P, T], F32, name=f"gate{t}_{r}")
+                nc.sync.dma_start(out=g[:], in_=gate[r, t * P : (t + 1) * P, :])
+                gates[t, r] = g
 
         x_codes = keep.tile([P, T], U32, name="x_codes", align_bytes=64)
         x_scales = keep.tile([P, T], U8, name="x_scales", align_bytes=64)
         nc.gpsimd.memset(x_scales[:], 0)
         x_grouped = keep.tile([P, T, PACK], BF16, name="x_grouped", align_bytes=64)
-        interleave(nc, x_grouped, x_raw, VECTOR_X, T)
+        v = VECTOR_TOKENS
+        interleave(nc.vector.tensor_copy, x_grouped[:, 0:v, :], x_raw[:, :, 0:v])
+        interleave(nc.scalar.copy, x_grouped[:, v:T, :], x_raw[:, :, v:T])
         nc.vector.quantize_mx(
             out=x_codes[:].bitcast(FP8X4),
             scales=x_scales[:],
@@ -102,40 +87,30 @@ def tile_routed_moe_kernel(tc, xT, w, b, gate, offs, pos1, pos2, out):
             nc.vector.tensor_copy(out=slot_scales[:, a:z], in_=x_scales[:].indirect(part))
 
         ys = [keep.tile([P, E * C], F32, name=f"y{t}") for t in range(BLOCKS)]
-        codes = {}
-        grouped = {}
+        w_grouped = [keep.tile([P, N, PACK], BF16, name=f"w_grouped{e}", align_bytes=64) for e in range(E)]
+        w_codes = [keep.tile([P, N], U32, name=f"w_codes{e}", align_bytes=64) for e in range(E)]
+        w_scales = [keep.tile([P, N], U8, name=f"w_scales{e}", align_bytes=64) for e in range(E)]
 
-        def convert(i):
-            e, f0, f1 = pieces[i]
-            width = f1 - f0
-            g = keep.tile([P, width, PACK], BF16, name=f"w_grouped{i}", align_bytes=64)
-            interleave(nc, g, raws[i], width * VECTOR_SHARES[i >= first_half] // 16, width)
-            grouped[i] = g
+        def convert(copy, e, a=0, z=N):
+            interleave(copy, w_grouped[e][:, a:z, :], raws[e][:, :, a:z])
 
-        def quantise(i):
-            e, f0, f1 = pieces[i]
-            width = f1 - f0
-            c = keep.tile([P, width], U32, name=f"w_codes{i}", align_bytes=64)
-            s = keep.tile([P, width], U8, name=f"w_scales{i}", align_bytes=64)
+        def quantise(e, a=0, z=N):
             nc.vector.quantize_mx(
-                out=c[:].bitcast(FP8X4),
-                scales=s[:],
-                in_=grouped[i][:].rearrange("p w j -> p (w j)"),
+                out=w_codes[e][:, a:z].bitcast(FP8X4),
+                scales=w_scales[e][:, a:z],
+                in_=w_grouped[e][:, a:z, :].rearrange("p w j -> p (w j)"),
             )
-            codes[i] = (c, s)
 
-        def multiply(i):
-            e, f0, f1 = pieces[i]
-            c, s = codes[i]
+        def multiply(e, a=0, z=N):
             slots = slice(e * C, (e + 1) * C)
-            for f in range(f0, f1, P):
+            for f in range(a, z, P):
                 t = f // P
-                cols = slice(f - f0, f - f0 + P)
+                cols = slice(f, f + P)
                 acc = psum.tile([P, C], F32, name="acc")
                 nc.tensor.matmul_mx(
                     out=acc[:],
-                    lhsT=c[:, cols].bitcast(FP8X4),
-                    lhsT_scale=s[:, cols],
+                    lhsT=w_codes[e][:, cols].bitcast(FP8X4),
+                    lhsT_scale=w_scales[e][:, cols],
                     rhs=slot_codes[:, slots].bitcast(FP8X4),
                     rhs_scale=slot_scales[:, slots],
                     start=True,
@@ -143,31 +118,44 @@ def tile_routed_moe_kernel(tc, xT, w, b, gate, offs, pos1, pos2, out):
                 )
                 nc.scalar.activation(ys[t][:, slots], acc[:], RELU, bias=bias[:, t, e : e + 1])
 
+        pieces = [(e, 0, N) for e in SCALAR_EXPERTS]
+        pieces += [(e, a, a + HALF) for e in range(len(SCALAR_EXPERTS), E) for a in (0, HALF)]
+        for piece in pieces[:2]:
+            convert(nc.scalar.copy, *piece)
+        for i in range(3):
+            gather(i)
+        for i in range(len(pieces) + 1):
+            if 2 <= i < len(pieces):
+                convert(nc.vector.tensor_copy, *pieces[i])
+            if i > 0:
+                quantise(*pieces[i - 1])
+                multiply(*pieces[i - 1])
+
+        products = {}
+
         def fetch(t, r):
             product = keep.tile([P, T], F32, name=f"product{t}_{r}")
             pos = (pos1_sb, pos2_sb)[r]
-            nc.vector.tensor_tensor(product[:], ys[t][:].indirect(pos[:]), gates[t][:, r, :], MULT)
+            nc.vector.tensor_tensor(product[:], ys[t][:].indirect(pos[:]), gates[t, r][:], MULT)
             products[t, r] = product
 
-        def finish(t):
-            total = keep.tile([P, T], F32, name=f"total{t}")
-            nc.vector.tensor_tensor(total[:], products[t, 0][:], products[t, 1][:], ADD)
-            nc.sync.dma_start(out=out[t * P : (t + 1) * P, :], in_=total[:])
+        totals = {}
 
-        products = {}
-        gather(0)
-        for i in range(E + 2):
-            if i < E:
-                convert(i)
-            if 1 <= i < len(GATHER_CUTS) - 1:
-                gather(i)
-            if 1 <= i <= E:
-                quantise(i - 1)
-            if i >= 2:
-                multiply(i - 2)
-        for t in range(BLOCKS):
+        def finish(t, a=0, z=T):
+            if t not in totals:
+                total = keep.tile([P, T], F32, name=f"total{t}")
+                totals[t] = total
+            total = totals[t]
+            nc.vector.tensor_tensor(total[:, a:z], products[t, 0][:, a:z], products[t, 1][:, a:z], ADD)
+            nc.sync.dma_start(out=out[t * P : (t + 1) * P, a:z], in_=total[:, a:z])
+
+        for t in range(BLOCKS - 1):
             fetch(t, 0)
             if t > 0:
                 finish(t - 1)
             fetch(t, 1)
-        finish(BLOCKS - 1)
+        fetch(BLOCKS - 1, 0)
+        fetch(BLOCKS - 1, 1)
+        finish(BLOCKS - 2)
+        finish(BLOCKS - 1, 0, T // 2)
+        finish(BLOCKS - 1, T // 2, T)

from contextlib import ExitStack

import concourse.mybir as mybir

F32 = mybir.dt.float32
BF16 = mybir.dt.bfloat16
U32 = mybir.dt.uint32
U16 = mybir.dt.uint16
U8 = mybir.dt.uint8
FP8X4 = mybir.dt.float8_e4m3fn_x4
MULT = mybir.AluOpType.mult
ADD = mybir.AluOpType.add
RELU = mybir.ActivationFunctionType.Relu

K, T, E, C, N = 512, 512, 8, 128, 512
FLOPS = 2 * K * N * E * C
P = 128
PACK = 4
BLOCKS = N // P

VECTOR_TOKENS = 320
SCALAR_EXPERTS = (0, 1)
HALF = N // 2
GATHER_CUTS = (0, 384, 768, 1024)


def interleave(copy, grouped, raw):
    copy(
        out=grouped.rearrange("p (c i) t -> p c t i", i=4),
        in_=raw.rearrange("p t (c i) -> p c t i", i=4),
    )


def tile_routed_moe_kernel(tc, xT, w, b, gate, offs, pos1, pos2, out):
    nc = tc.nc
    with ExitStack() as ctx:
        lists = ctx.enter_context(tc.tile_pool(name="lists", bufs=1))
        keep = ctx.enter_context(tc.tile_pool(name="keep", bufs=1))
        psum = ctx.enter_context(tc.psum_pool(name="psum", bufs=8))

        offs_sb = lists.tile([P, E * C // 16], U16, name="offs_sb")
        pos1_sb = lists.tile([P, T // 16], U16, name="pos1_sb")
        pos2_sb = lists.tile([P, T // 16], U16, name="pos2_sb")
        bias = lists.tile([P, BLOCKS, E], F32, name="bias")

        x_raw = keep.tile([P, PACK, T], F32, name="x_raw")
        nc.sync.dma_start(out=x_raw[:], in_=xT.rearrange("(p j) w -> p j w", j=PACK))
        nc.sync.dma_start(out=offs_sb[:], in_=offs)
        raws = []
        for e in range(E):
            raw = keep.tile([P, PACK, N], F32, name=f"w_raw{e}")
            rows = w[e].rearrange("(p j) n -> p j n", j=PACK)
            for a, z in ((0, HALF), (HALF, N)) if e == E - 1 else ((0, N),):
                nc.sync.dma_start(out=raw[:, :, a:z], in_=rows[:, :, a:z])
            raws.append(raw)
            if e == 0:
                nc.sync.dma_start(out=bias[:], in_=b.rearrange("(t p) e -> p t e", p=P))
            if e == E - 2:
                nc.sync.dma_start(out=pos1_sb[:], in_=pos1)
                nc.sync.dma_start(out=pos2_sb[:], in_=pos2)
        gates = {}
        for t in range(BLOCKS):
            for r in range(2):
                g = keep.tile([P, T], F32, name=f"gate{t}_{r}")
                nc.sync.dma_start(out=g[:], in_=gate[r, t * P : (t + 1) * P, :])
                gates[t, r] = g

        x_codes = keep.tile([P, T], U32, name="x_codes", align_bytes=64)
        x_scales = keep.tile([P, T], U8, name="x_scales", align_bytes=64)
        nc.gpsimd.memset(x_scales[:], 0)
        x_grouped = keep.tile([P, T, PACK], BF16, name="x_grouped", align_bytes=64)
        v = VECTOR_TOKENS
        interleave(nc.vector.tensor_copy, x_grouped[:, 0:v, :], x_raw[:, :, 0:v])
        interleave(nc.scalar.copy, x_grouped[:, v:T, :], x_raw[:, :, v:T])
        nc.vector.quantize_mx(
            out=x_codes[:].bitcast(FP8X4),
            scales=x_scales[:],
            in_=x_grouped[:].rearrange("p w j -> p (w j)"),
        )
        slot_codes = keep.tile([P, E * C], U32, name="slot_codes", align_bytes=64)
        slot_scales = keep.tile([P, E * C], U8, name="slot_scales", align_bytes=64)

        def gather(i):
            a, z = GATHER_CUTS[i], GATHER_CUTS[i + 1]
            part = offs_sb[:, a // 16 : z // 16]
            nc.vector.tensor_copy(out=slot_codes[:, a:z], in_=x_codes[:].indirect(part))
            nc.vector.tensor_copy(out=slot_scales[:, a:z], in_=x_scales[:].indirect(part))

        ys = [keep.tile([P, E * C], F32, name=f"y{t}") for t in range(BLOCKS)]
        w_grouped = [keep.tile([P, N, PACK], BF16, name=f"w_grouped{e}", align_bytes=64) for e in range(E)]
        w_codes = [keep.tile([P, N], U32, name=f"w_codes{e}", align_bytes=64) for e in range(E)]
        w_scales = [keep.tile([P, N], U8, name=f"w_scales{e}", align_bytes=64) for e in range(E)]

        def convert(copy, e, a=0, z=N):
            interleave(copy, w_grouped[e][:, a:z, :], raws[e][:, :, a:z])

        def quantise(e, a=0, z=N):
            nc.vector.quantize_mx(
                out=w_codes[e][:, a:z].bitcast(FP8X4),
                scales=w_scales[e][:, a:z],
                in_=w_grouped[e][:, a:z, :].rearrange("p w j -> p (w j)"),
            )

        def multiply(e, a=0, z=N):
            slots = slice(e * C, (e + 1) * C)
            for f in range(a, z, P):
                t = f // P
                cols = slice(f, f + P)
                acc = psum.tile([P, C], F32, name="acc")
                nc.tensor.matmul_mx(
                    out=acc[:],
                    lhsT=w_codes[e][:, cols].bitcast(FP8X4),
                    lhsT_scale=w_scales[e][:, cols],
                    rhs=slot_codes[:, slots].bitcast(FP8X4),
                    rhs_scale=slot_scales[:, slots],
                    start=True,
                    stop=True,
                )
                nc.scalar.activation(ys[t][:, slots], acc[:], RELU, bias=bias[:, t, e : e + 1])

        pieces = [(e, 0, N) for e in SCALAR_EXPERTS]
        pieces += [(e, a, a + HALF) for e in range(len(SCALAR_EXPERTS), E) for a in (0, HALF)]
        for piece in pieces[:2]:
            convert(nc.scalar.copy, *piece)
        for i in range(3):
            gather(i)
        for i in range(len(pieces) + 1):
            if 2 <= i < len(pieces):
                convert(nc.vector.tensor_copy, *pieces[i])
            if i > 0:
                quantise(*pieces[i - 1])
                multiply(*pieces[i - 1])

        products = {}

        def fetch(t, r):
            product = keep.tile([P, T], F32, name=f"product{t}_{r}")
            pos = (pos1_sb, pos2_sb)[r]
            nc.vector.tensor_tensor(product[:], ys[t][:].indirect(pos[:]), gates[t, r][:], MULT)
            products[t, r] = product

        totals = {}

        def finish(t, a=0, z=T):
            if t not in totals:
                total = keep.tile([P, T], F32, name=f"total{t}")
                totals[t] = total
            total = totals[t]
            nc.vector.tensor_tensor(total[:, a:z], products[t, 0][:, a:z], products[t, 1][:, a:z], ADD)
            nc.sync.dma_start(out=out[t * P : (t + 1) * P, a:z], in_=total[:, a:z])

        for t in range(BLOCKS - 1):
            fetch(t, 0)
            if t > 0:
                finish(t - 1)
            fetch(t, 1)
        fetch(BLOCKS - 1, 0)
        fetch(BLOCKS - 1, 1)
        finish(BLOCKS - 2)
        finish(BLOCKS - 1, 0, T // 2)
        finish(BLOCKS - 1, T // 2, T)
